import numpy as np
import ml_dtypes


def mxq(x, axis, fmt="e4m3"):
    dtype, down = {"e4m3": (ml_dtypes.float8_e4m3fn, 7), "e5m2": (ml_dtypes.float8_e5m2, 14)}[fmt]
    v = np.moveaxis(np.asarray(x, np.float32).astype(ml_dtypes.bfloat16).astype(np.float64), axis, -1)
    blocks = v.reshape(v.shape[:-1] + (-1, 32))
    amax = np.abs(blocks).max(-1, keepdims=True)
    byte = np.maximum(np.where(amax > 0, np.frexp(amax)[1] - 1 + 127, 0) - down, 1)
    scale = np.exp2(byte - 127.0)
    codes = (blocks / scale).astype(np.float32).astype(dtype).astype(np.float64)
    return np.moveaxis((codes * scale).reshape(v.shape), -1, axis)


WIDE = False


def mx_kscale(k):
    if not WIDE:
        return np.ones(k)
    levels = np.array([10, -10, 5, -5, 0])
    if k % 512:
        return np.exp2(np.random.permutation(np.resize(levels, k // 32))).repeat(32)
    a = np.empty((k // 512, 16))
    for p in range(k // 512):
        a[p, :8] = np.random.permutation(np.resize(levels, 8))
        for g in range(8):
            far = levels[np.abs(levels - a[p, g]) >= 10]
            a[p, g + 8] = far[np.random.randint(len(far))]
    return np.exp2(a.ravel()).repeat(32)


def f64(x):
    return np.asarray(x).astype(np.float64)


def striped(idx):
    return np.tile(idx.reshape(-1, 16).T, (8, 1)).astype(np.uint16)


def unstriped(offs):
    return offs[:16].T.reshape(-1).astype(np.int64)


def striped8(idx):
    return np.concatenate([x.reshape(-1, 16).T for x in idx]).astype(np.uint16)


def runs(offs, k):
    lists = np.stack([offs[16 * r : 16 * r + 16].T.reshape(-1) for r in range(8)]).astype(np.int64)
    return lists[np.arange(k) % 512 // 64]


def pack_weight(w):
    k, n = w.shape
    w = f64(np.asarray(w, np.float32).astype(ml_dtypes.bfloat16)).reshape(k // 32, 32, n)
    amax = np.abs(w).max(1)
    byte = np.clip(np.where(amax > 0, np.frexp(amax)[1] - 1 + 127 - 7, 1), 1, 254)
    scaled = (w * np.exp2(127.0 - byte)[:, None, :]).reshape(k, n).astype(np.float32)
    words = np.ascontiguousarray(scaled.reshape(k // 512, 128, 4, n).transpose(0, 1, 3, 2)).astype(ml_dtypes.float8_e4m3fn).view(np.uint8)
    return words, np.ascontiguousarray(byte.astype(np.uint8).reshape(k // 512, 16, n))


def unpack_weight(words, scales):
    g, p, n, _ = words.shape
    vals = np.ascontiguousarray(words).view(ml_dtypes.float8_e4m3fn).astype(np.float64) * np.repeat(np.exp2(scales.astype(np.float64) - 127.0), 8, axis=1)[..., None]
    return vals.transpose(0, 1, 3, 2).reshape(g * 512, n)


E2M1 = np.array([0.0, 0.5, 1.0, 1.5, 2.0, 3.0, 4.0, 6.0, -0.0, -0.5, -1.0, -1.5, -2.0, -3.0, -4.0, -6.0])


def pack_fp4(w):
    k, n = w.shape
    w = f64(np.asarray(w, np.float32).astype(ml_dtypes.bfloat16)).reshape(k // 32, 32, n)
    amax = np.abs(w).max(1)
    mant, ex = np.frexp(amax / 6.0)
    byte = np.clip(np.where(amax > 0, np.where(mant > 0.5, ex, ex - 1) + 127, 1), 1, 254)
    scaled = (w * np.exp2(127.0 - byte)[:, None, :]).reshape(k, n).astype(np.float32)
    c = np.ascontiguousarray(scaled.reshape(k // 512, 128, 4, n).transpose(0, 1, 3, 2)).astype(ml_dtypes.float4_e2m1fn).view(np.uint8) & 0xF
    words = (c[..., 0::2] | (c[..., 1::2] << 4)).reshape(k // 512, 128, 2 * n)
    return np.ascontiguousarray(words), np.ascontiguousarray(byte.astype(np.uint8).reshape(k // 512, 16, n))


def unpack_fp4(words, scales):
    g, _, n = scales.shape
    words = np.ascontiguousarray(words).reshape(g, 128, n, 2)
    nib = np.empty((g, 128, n, 4), np.uint8)
    nib[..., 0::2] = words & 0xF
    nib[..., 1::2] = words >> 4
    vals = E2M1[nib] * np.repeat(np.exp2(scales.astype(np.float64) - 127.0), 8, axis=1)[..., None]
    return vals.transpose(0, 1, 3, 2).reshape(g * 512, n)


def planes(y):
    n, m = y.shape
    v = y.astype(np.float32).astype(ml_dtypes.bfloat16).astype(np.float64).reshape(n // 32, 32, m)
    top = np.abs(v).max(1)
    byte = np.clip(np.where(top > 0, np.frexp(top)[1] - 1 + 127 - 7, 1), 1, 254)
    codes = (v * np.exp2(127.0 - byte)[:, None, :]).reshape(n, m).astype(np.float32).astype(ml_dtypes.float8_e4m3fn).view(np.uint8)
    words = codes.reshape(n // 512, 128, 4, m).transpose(0, 1, 3, 2)
    return np.ascontiguousarray(words), np.ascontiguousarray(byte.astype(np.uint8).reshape(n // 512, 16, m))


K, T, S, N, G, H = 512, 2048, 256, 512, 2048, 512


def setup_inputs():
    n = np.random.standard_normal
    s = mx_kscale(K)[:, None]
    u = mx_kscale(K)
    packed_xT = pack_weight(n((K, T)) * s)
    packed_dT = pack_weight(n((K, G)) / s)
    packed_w1 = pack_fp4(n((H, N)) / np.sqrt(H) / u[:, None])
    return {
        "x_words": packed_xT[0],
        "x_scales": packed_xT[1],
        "d_words": packed_dT[0],
        "d_scales": packed_dT[1],
        "gn": (np.random.uniform(0.5, 1.5, (H, 1)) * u[:, None]).astype(np.float32),
        "w1_words": packed_w1[0],
        "w1_scales": packed_w1[1],
        "offs": striped(np.random.permutation(T)[:S]),
        "k1": striped8(np.random.randint(0, G, (8, H))),
        "two": striped(np.random.permutation(T)[:S]),
        "n1": striped(np.random.permutation(S)),
        "n2": striped(np.random.permutation(S)),
        "n3": striped8(np.stack([np.random.permutation(S) for _ in range(8)])),
        "n4": striped8(np.stack([np.random.permutation(S) for _ in range(8)])),
    }


def reference(x_words, x_scales, d_words, d_scales, gn, w1_words, w1_scales, offs, k1, two, n1, n2, n3, n4):
    d_k1 = unpack_weight(d_words, d_scales)[np.arange(K)[:, None], runs(k1, K)]
    xq = unpack_weight(x_words, x_scales)[:, unstriped(offs)]
    a = 0.0625 * (d_k1.T @ xq)
    x_two = unpack_weight(x_words, x_scales)[:, unstriped(two)]
    b = 0.0625 * (d_k1.T @ x_two)
    z = f64(gn) * (np.maximum(a, b[:, unstriped(n2)]) - (np.minimum(a[:, unstriped(n1)], b)))
    h = unpack_fp4(w1_words, w1_scales).T @ mxq(z, 0, "e4m3")
    out_0 = np.maximum(h[np.arange(N)[:, None], runs(n3, N)], h[np.arange(N)[:, None], runs(n4, N)]) - (0.75 * h)
    return (out_0,) + planes(out_0)

@@ -1,0 +1,267 @@
+from contextlib import ExitStack
+
+import concourse.mybir as mybir
+
+K, T, S, N, G, H = 512, 2048, 256, 512, 2048, 512
+FLOPS = 2 * K * H * S * 2 + 2 * H * N * S
+
+F32 = mybir.dt.float32
+BF16 = mybir.dt.bfloat16
+I32 = mybir.dt.int32
+U32 = mybir.dt.uint32
+U16 = mybir.dt.uint16
+U8 = mybir.dt.uint8
+FP8X4 = mybir.dt.float8_e4m3fn_x4
+FP4X4 = mybir.dt.float4_e2m1fn_x4
+ALU = mybir.AluOpType
+COPY = mybir.ActivationFunctionType.Copy
+
+P = 128
+
+
+def tile_picked_twksmaxbover_none_po_kernel(
+    tc, x_words, x_scales, d_words, d_scales, gn, w1_words, w1_scales, offs, k1, two, n1, n2, n3, n4, out_0, out_1, out_2
+):
+    nc = tc.nc
+    with ExitStack() as ctx:
+        sb = ctx.enter_context(tc.tile_pool(name="sb", bufs=1))
+        ps = ctx.enter_context(tc.psum_pool(name="ps", bufs=1))
+
+        def tile(name, cols, dtype, tag=None):
+            return sb.tile([P, cols], dtype, name=name, tag=tag or name, align_bytes=64)
+
+        def load_list(name, src):
+            t = sb.tile([P, src.shape[1]], U16, name=name)
+            nc.sync.dma_start(t[:], src)
+            return t
+
+        d_win = tile("d_win", G, U32)
+        x_win = tile("x_win", T, U32)
+        ds_win = tile("ds_win", G, U8)
+        xs_win = tile("xs_win", T, U8)
+        planes = tile("planes", H + 2 * S, U8)
+        w1s_raw = tile("w1s_raw", N, U8)
+
+        nc.vector.memset(ds_win[:].bitcast(I32), 0)
+        nc.vector.memset(xs_win[:].bitcast(I32), 0)
+        nc.vector.memset(w1s_raw[:].bitcast(I32), 0)
+        nc.vector.memset(planes[:].bitcast(I32), 0)
+        nc.gpsimd.dma_start(ds_win[0:P:8, :].bitcast(I32), d_scales[0].bitcast(I32))
+        nc.gpsimd.dma_start(xs_win[0:P:8, :].bitcast(I32), x_scales[0].bitcast(I32))
+        nc.scalar.dma_start(d_win[:].bitcast(I32), d_words[0].rearrange("p n t -> p (n t)").bitcast(I32))
+        k1_t = load_list("k1_t", k1)
+        offs_t = load_list("offs_t", offs)
+        two_t = load_list("two_t", two)
+        n1_t = load_list("n1_t", n1)
+        n2_t = load_list("n2_t", n2)
+        n3_t = load_list("n3_t", n3)
+        nc.sync.dma_start(x_win[:].bitcast(I32), x_words[0].rearrange("p n t -> p (n t)").bitcast(I32))
+        n4_t = load_list("n4_t", n4)
+
+        picked_s = tile("picked_s", H + 2 * S, U8)
+        nc.vector.tensor_copy(picked_s[:, 0:H], ds_win[:].indirect(k1_t[:]))
+        nc.vector.tensor_copy(picked_s[:, H : H + S], xs_win[:].indirect(offs_t[:]))
+        nc.vector.tensor_copy(picked_s[:, H + S :], xs_win[:].indirect(two_t[:]))
+        for i in range(4):
+            nc.scalar.dma_start(planes[i:P:32, :].bitcast(I32), picked_s[8 * i : P : 32, :].bitcast(I32))
+
+        d_picked = tile("d_picked", H, U32, tag="xs_win")
+        nc.vector.tensor_copy(d_picked[:], d_win[:].indirect(k1_t[:]))
+        keys = tile("keys", H, U32)
+        nc.vector.tensor_copy(keys[:].rearrange("p (t m) -> p m t", t=4), d_picked[:].rearrange("p (m t) -> p m t", t=4))
+        xa = tile("xa", S, U32, tag="xs_win")
+        nc.vector.tensor_copy(xa[:], x_win[:].indirect(offs_t[:]))
+        keys_s = tile("keys_s", H, U8)
+        nc.vector.tensor_copy(keys_s[:].rearrange("p (t m) -> p m t", t=4), planes[:, 0:H].rearrange("p (m t) -> p m t", t=4))
+        xb = tile("xb", S, U32)
+        nc.vector.tensor_copy(xb[:], x_win[:].indirect(two_t[:]))
+
+        w1w_raw = tile("w1w_raw", 2 * N, U8, tag="ds_win")
+        gain = tile("gain", 4, F32, tag="picked_s")
+        nc.gpsimd.dma_start(w1w_raw[:].bitcast(I32), w1_words[0].bitcast(I32))
+        for q in range(4):
+            nc.gpsimd.dma_start(w1s_raw[32 * q : 32 * q + 4, :].bitcast(I32), w1_scales[0, 4 * q : 4 * q + 4, :].bitcast(I32))
+        nc.gpsimd.dma_start(gain[:], gn.rearrange("(p t) o -> p (t o)", t=4))
+
+        a_ps = [ps.tile([P, 2 * S], F32, name=f"a_ps{u}") for u in range(2)]
+        b_ps = [ps.tile([P, 2 * S], F32, name=f"b_ps{u}") for u in range(2)]
+        for u in range(2):
+            for bank, tokens, first in ((a_ps[u], xa, H), (b_ps[u], xb, H + S)):
+                for e in range(2):
+                    cols = slice(P * (2 * u + e), P * (2 * u + e + 1))
+                    nc.tensor.matmul_mx(
+                        out=bank[:, S * e : S * (e + 1)],
+                        lhsT=keys[:, cols].bitcast(FP8X4),
+                        lhsT_scale=keys_s[:, cols],
+                        rhs=tokens[:].bitcast(FP8X4),
+                        rhs_scale=planes[:, first : first + S],
+                        start=True,
+                        stop=True,
+                    )
+
+        w1w = [tile("w1w_first", 2 * P, U8, tag="x_win")[:]]
+        w1s = [tile("w1s_first", P, U8, tag="xs_win")[:]]
+
+        def deal_w1(t):
+            nc.vector.tensor_copy(
+                w1w[t].rearrange("p (m b) -> p m b", b=2),
+                w1w_raw[:].rearrange("p (m t b) -> p m t b", t=4, b=2)[:, :, t, :],
+            )
+            nc.vector.tensor_copy(w1s[t], w1s_raw[:].rearrange("p (m t) -> p m t", t=4)[:, :, t])
+
+        deal_w1(0)
+
+        a_sb = [tile(f"a_sb{u}", 3 * S, F32) for u in range(2)]
+        b_sb = [tile(f"b_sb{u}", 3 * S, F32) for u in range(2)]
+        a_n1 = [tile(f"a_n1_{u}", 2 * S, F32) for u in range(2)]
+        b_n2 = [tile(f"b_n2_{u}", 2 * S, F32) for u in range(2)]
+        larger = tile("larger", 4 * S, F32)
+        smaller = tile("smaller", 4 * S, F32)
+        diff = tile("diff", 4 * S, F32)
+        z = tile("z", 4 * S, BF16)
+        z_codes = tile("z_codes", S, U32)
+        z_scales = tile("z_scales", S, U8)
+        h_sb = [tile(f"h_sb{t}", 2 * S, F32) for t in range(4)]
+        HALF = S // 2
+
+        def fetch(engine, dst, src, lst, t, lo, hi):
+            u, e = divmod(t, 2)
+            window = src[u][:, S * e : S * (e + 2)].indirect(lst[:, lo // 16 : hi // 16])
+            out = dst[u][:, S * e + lo : S * e + hi]
+            if engine is nc.vector:
+                nc.vector.tensor_copy(out, window)
+            else:
+                nc.scalar.activation(out, window, COPY)
+
+        def part(ap, u, lo, hi):
+            return ap[:, 0 : 2 * S].rearrange("p (e j) -> p e j", e=2)[:, :, lo:hi]
+
+        def wide(t_, u, lo, hi):
+            return t_[:, 2 * S * u : 2 * S * (u + 1)].rearrange("p (e j) -> p e j", e=2)[:, :, lo:hi]
+
+        def take_max(u, lo, hi):
+            nc.vector.tensor_tensor(wide(larger, u, lo, hi), part(a_sb[u], u, lo, hi), part(b_n2[u], u, lo, hi), ALU.max)
+
+        def take_min(u, lo, hi):
+            nc.vector.tensor_tensor(wide(smaller, u, lo, hi), part(a_n1[u], u, lo, hi), part(b_sb[u], u, lo, hi), ALU.min)
+
+        def take_diff(u, lo, hi):
+            nc.vector.tensor_tensor(wide(diff, u, lo, hi), wide(larger, u, lo, hi), wide(smaller, u, lo, hi), ALU.subtract)
+
+        def round_z(lo, hi):
+            nc.vector.tensor_tensor(
+                z[:, 4 * lo : 4 * hi].rearrange("p (c i t) -> p c t i", i=4, t=4),
+                diff[:].rearrange("p (t c i) -> p c t i", i=4, t=4)[:, lo // 4 : hi // 4, :, :],
+                gain[:].unsqueeze(1).unsqueeze(3).to_broadcast([P, (hi - lo) // 4, 4, 4]),
+                ALU.mult,
+            )
+
+        def quantise_z(lo, hi):
+            nc.vector.quantize_mx(out=z_codes[:, lo:hi].bitcast(FP8X4), scales=z_scales[:, lo:hi], in_=z[:, 4 * lo : 4 * hi])
+
+        def layer(t, lo, hi, tag):
+            h_ps = ps.tile([P, hi - lo], F32, name=f"h_ps{t}_{lo}", tag=tag)
+            nc.tensor.matmul_mx(
+                out=h_ps[:],
+                lhsT=w1w[t].bitcast(FP4X4),
+                lhsT_scale=w1s[t],
+                rhs=z_codes[:, lo:hi].bitcast(FP8X4),
+                rhs_scale=z_scales[:, lo:hi],
+                start=True,
+                stop=True,
+            )
+            return h_ps
+
+        nc.scalar.activation(a_sb[0][:, 0 : 2 * S], a_ps[0][:], COPY, scale=0.0625)
+        nc.vector.tensor_scalar(b_sb[0][:, 0 : 2 * S], b_ps[0][:], 0.0625, None, ALU.mult)
+        nc.scalar.activation(a_sb[1][:, 0 : 2 * S], a_ps[1][:], COPY, scale=0.0625)
+        fetch(nc.vector, a_n1, a_sb, n1_t, 0, 0, S)
+        nc.vector.tensor_scalar(b_sb[1][:, 0 : 2 * S], b_ps[1][:], 0.0625, None, ALU.mult)
+        fetch(nc.scalar, a_n1, a_sb, n1_t, 1, 0, S)
+        fetch(nc.scalar, b_n2, b_sb, n2_t, 0, 0, S)
+        fetch(nc.scalar, b_n2, b_sb, n2_t, 1, 0, S)
+        take_min(0, 0, S)
+        take_max(0, 0, S)
+        for lo in (0, HALF):
+            for t in (2, 3):
+                fetch(nc.scalar, a_n1, a_sb, n1_t, t, lo, lo + HALF)
+            for t in (2, 3):
+                fetch(nc.scalar, b_n2, b_sb, n2_t, t, lo, lo + HALF)
+        take_min(1, 0, HALF)
+        take_diff(0, 0, S)
+        take_max(1, 0, HALF)
+        take_min(1, HALF, S)
+        take_diff(1, 0, HALF)
+        take_max(1, HALF, S)
+        round_z(0, HALF)
+        take_diff(1, HALF, S)
+        quantise_z(0, HALF)
+        round_z(HALF, S)
+        h_ps = layer(0, 0, HALF, "h0_lo")
+        nc.scalar.copy(h_sb[0][:, 0:HALF], h_ps[:])
+        quantise_z(HALF, S)
+        h_ps = layer(0, HALF, S, "h0_hi")
+        nc.scalar.copy(h_sb[0][:, HALF:S], h_ps[:])
+        w1w_rest = tile("w1w_rest", 6 * P, U8, tag="diff")
+        w1s_rest = tile("w1s_rest", 3 * P, U8, tag="picked_s")
+        for t in range(1, 4):
+            w1w.append(w1w_rest[:, 2 * P * (t - 1) : 2 * P * t])
+            w1s.append(w1s_rest[:, P * (t - 1) : P * t])
+            deal_w1(t)
+            h_ps = layer(t, 0, S, ["", "h1", "h2", "a_ps0"][t])
+            nc.vector.tensor_copy(h_sb[t][:, 0:S], h_ps[:])
+
+        y = tile("y", 4 * S, F32)
+        y_bf = tile("y_bf", 4 * S, BF16)
+        y_codes = tile("y_codes", S, U32)
+        y_scales = tile("y_scales", S, U8)
+        h_n3 = tile("h_n3", 4 * S, F32)
+        h_n4 = tile("h_n4", 4 * S, F32)
+        top = tile("top", 4 * S, F32)
+        out_rows = out_0.rearrange("(p t) j -> p t j", t=4)
+        out_words = out_1[0].rearrange("p n t -> p (n t)").bitcast(I32)
+
+        def fetch_h(t, lo, hi):
+            cols = slice(S * t + lo, S * t + hi)
+            nc.scalar.activation(h_n3[:, cols], h_sb[t][:].indirect(n3_t[:, lo // 16 : hi // 16]), COPY)
+            nc.scalar.activation(h_n4[:, cols], h_sb[t][:].indirect(n4_t[:, lo // 16 : hi // 16]), COPY)
+
+        def take_top(t, lo, hi):
+            cols = slice(S * t + lo, S * t + hi)
+            nc.vector.tensor_tensor(top[:, cols], h_n3[:, cols], h_n4[:, cols], ALU.max)
+
+        def take_y(t, lo, hi):
+            cols = slice(S * t + lo, S * t + hi)
+            nc.vector.scalar_tensor_tensor(y[:, cols], h_sb[t][:, lo:hi], -0.75, top[:, cols], ALU.mult, ALU.add)
+
+        def round_y(t, lo, hi):
+            nc.vector.tensor_copy(
+                y_bf[:].rearrange("p (j t) -> p j t", t=4)[:, lo:hi, t : t + 2],
+                y[:].rearrange("p (t j) -> p j t", t=4)[:, lo:hi, t : t + 2],
+            )
+
+        def quantise_y(lo, hi):
+            nc.vector.quantize_mx(out=y_codes[:, lo:hi].bitcast(FP8X4), scales=y_scales[:, lo:hi], in_=y_bf[:, 4 * lo : 4 * hi])
+            nc.sync.dma_start(out_words[:, lo:hi], y_codes[:, lo:hi].bitcast(I32))
+
+        for t in range(3):
+            fetch_h(t, 0, S)
+            take_top(t, 0, S)
+            take_y(t, 0, S)
+            nc.sync.dma_start(out_rows[:, t, :], y[:, S * t : S * (t + 1)])
+            if t == 1:
+                round_y(0, 0, S)
+        fetch_h(3, 0, HALF)
+        fetch_h(3, HALF, S)
+        take_top(3, 0, HALF)
+        take_y(3, 0, HALF)
+        take_top(3, HALF, S)
+        round_y(2, 0, HALF)
+        take_y(3, HALF, S)
+        nc.scalar.dma_start(out_rows[:, 3, :], y[:, S * 3 : S * 4])
+        quantise_y(0, HALF)
+        round_y(2, HALF, S)
+        quantise_y(HALF, S)
+        for q in range(4):
+            queue = nc.scalar if q % 2 == 0 else nc.sync
+            queue.dma_start(out_2[0, 4 * q : 4 * q + 4, :].bitcast(I32), y_scales[32 * q : 32 * q + 4, :].bitcast(I32))

@@ -40,30 +40,31 @@ def tile_picked_twksmaxbover_none_po_kernel(
         ds_win = tile("ds_win", G, U8)
         xs_win = tile("xs_win", T, U8)
         planes = tile("planes", H + 2 * S, U8)
-        w1s_raw = tile("w1s_raw", N, U8)
 
-        nc.vector.memset(ds_win[:].bitcast(I32), 0)
-        nc.vector.memset(xs_win[:].bitcast(I32), 0)
-        nc.vector.memset(w1s_raw[:].bitcast(I32), 0)
-        nc.vector.memset(planes[:].bitcast(I32), 0)
-        nc.gpsimd.dma_start(ds_win[0:P:8, :].bitcast(I32), d_scales[0].bitcast(I32))
-        nc.gpsimd.dma_start(xs_win[0:P:8, :].bitcast(I32), x_scales[0].bitcast(I32))
-        nc.scalar.dma_start(d_win[:].bitcast(I32), d_words[0].rearrange("p n t -> p (n t)").bitcast(I32))
+        def spread(scales):
+            rows = scales[0].bitcast(I32)
+            return rows.unsqueeze(1).to_broadcast([16, 8, rows.shape[1]])
+
+        nc.sync.dma_start(ds_win[:].bitcast(I32), spread(d_scales))
         k1_t = load_list("k1_t", k1)
+        nc.sync.dma_start(xs_win[:].bitcast(I32), spread(x_scales))
         offs_t = load_list("offs_t", offs)
         two_t = load_list("two_t", two)
         n1_t = load_list("n1_t", n1)
         n2_t = load_list("n2_t", n2)
-        n3_t = load_list("n3_t", n3)
+        nc.sync.dma_start(d_win[:].bitcast(I32), d_words[0].rearrange("p n t -> p (n t)").bitcast(I32))
         nc.sync.dma_start(x_win[:].bitcast(I32), x_words[0].rearrange("p n t -> p (n t)").bitcast(I32))
+        n3_t = load_list("n3_t", n3)
         n4_t = load_list("n4_t", n4)
+        nc.vector.memset(planes[:].bitcast(I32), 0)
 
-        picked_s = tile("picked_s", H + 2 * S, U8)
-        nc.vector.tensor_copy(picked_s[:, 0:H], ds_win[:].indirect(k1_t[:]))
-        nc.vector.tensor_copy(picked_s[:, H : H + S], xs_win[:].indirect(offs_t[:]))
-        nc.vector.tensor_copy(picked_s[:, H + S :], xs_win[:].indirect(two_t[:]))
+        staged = tile("staged", H + 2 * S, U8)
+        nc.vector.tensor_copy(staged[:, 0:H], ds_win[:].indirect(k1_t[:]))
+        nc.vector.tensor_copy(staged[:, H : H + S], xs_win[:].indirect(offs_t[:]))
+        nc.vector.tensor_copy(staged[:, H + S :], xs_win[:].indirect(two_t[:]))
         for i in range(4):
-            nc.scalar.dma_start(planes[i:P:32, :].bitcast(I32), picked_s[8 * i : P : 32, :].bitcast(I32))
+            queue = nc.scalar if i % 2 == 0 else nc.sync
+            queue.dma_start(planes[i:P:32, :].bitcast(I32), staged[8 * i : P : 32, :].bitcast(I32))
 
         d_picked = tile("d_picked", H, U32, tag="xs_win")
         nc.vector.tensor_copy(d_picked[:], d_win[:].indirect(k1_t[:]))
@@ -72,15 +73,25 @@ def tile_picked_twksmaxbover_none_po_kernel(
         xa = tile("xa", S, U32, tag="xs_win")
         nc.vector.tensor_copy(xa[:], x_win[:].indirect(offs_t[:]))
         keys_s = tile("keys_s", H, U8)
-        nc.vector.tensor_copy(keys_s[:].rearrange("p (t m) -> p m t", t=4), planes[:, 0:H].rearrange("p (m t) -> p m t", t=4))
+
+        def deal_key_scales(u):
+            nc.vector.tensor_copy(
+                keys_s[:, 2 * P * u : 2 * P * (u + 1)].rearrange("p (e m) -> p m e", e=2),
+                planes[:, 0:H].rearrange("p (m t) -> p m t", t=4)[:, :, 2 * u : 2 * u + 2],
+            )
+
+        deal_key_scales(0)
         xb = tile("xb", S, U32)
         nc.vector.tensor_copy(xb[:], x_win[:].indirect(two_t[:]))
+        deal_key_scales(1)
 
-        w1w_raw = tile("w1w_raw", 2 * N, U8, tag="ds_win")
-        gain = tile("gain", 4, F32, tag="picked_s")
-        nc.gpsimd.dma_start(w1w_raw[:].bitcast(I32), w1_words[0].bitcast(I32))
+        w1w_raw = tile("w1w_raw", 2 * N, U8, tag="d_win")
+        w1s_raw = tile("w1s_raw", N, U8, tag="staged")
+        gain = tile("gain", 4, F32)
+        nc.gpsimd.memset(w1s_raw[:].bitcast(I32), 0)
         for q in range(4):
-            nc.gpsimd.dma_start(w1s_raw[32 * q : 32 * q + 4, :].bitcast(I32), w1_scales[0, 4 * q : 4 * q + 4, :].bitcast(I32))
+            nc.sync.dma_start(w1s_raw[32 * q : 32 * q + 4, :].bitcast(I32), w1_scales[0, 4 * q : 4 * q + 4, :].bitcast(I32))
+        nc.sync.dma_start(w1w_raw[:].bitcast(I32), w1_words[0].bitcast(I32))
         nc.gpsimd.dma_start(gain[:], gn.rearrange("(p t) o -> p (t o)", t=4))
 
         a_ps = [ps.tile([P, 2 * S], F32, name=f"a_ps{u}") for u in range(2)]
@@ -203,7 +214,7 @@ def tile_picked_twksmaxbover_none_po_kernel(
         h_ps = layer(0, HALF, S, "h0_hi")
         nc.scalar.copy(h_sb[0][:, HALF:S], h_ps[:])
         w1w_rest = tile("w1w_rest", 6 * P, U8, tag="diff")
-        w1s_rest = tile("w1s_rest", 3 * P, U8, tag="picked_s")
+        w1s_rest = tile("w1s_rest", 3 * P, U8, tag="gain")
         for t in range(1, 4):
             w1w.append(w1w_rest[:, 2 * P * (t - 1) : 2 * P * t])
             w1s.append(w1s_rest[:, P * (t - 1) : P * t])

@@ -41,13 +41,11 @@ def tile_picked_twksmaxbover_none_po_kernel(
         xs_win = tile("xs_win", T, U8)
         planes = tile("planes", H + 2 * S, U8)
 
-        def spread(scales):
-            rows = scales[0].bitcast(I32)
-            return rows.unsqueeze(1).to_broadcast([16, 8, rows.shape[1]])
-
-        nc.sync.dma_start(ds_win[:].bitcast(I32), spread(d_scales))
+        nc.vector.memset(ds_win[:].bitcast(I32), 0)
+        nc.gpsimd.memset(xs_win[:].bitcast(I32), 0)
         k1_t = load_list("k1_t", k1)
-        nc.sync.dma_start(xs_win[:].bitcast(I32), spread(x_scales))
+        nc.scalar.dma_start(ds_win[0:P:8, :].bitcast(I32), d_scales[0].bitcast(I32))
+        nc.scalar.dma_start(xs_win[0:P:8, :].bitcast(I32), x_scales[0].bitcast(I32))
         offs_t = load_list("offs_t", offs)
         two_t = load_list("two_t", two)
         n1_t = load_list("n1_t", n1)
@@ -63,16 +61,15 @@ def tile_picked_twksmaxbover_none_po_kernel(
         nc.vector.tensor_copy(staged[:, H : H + S], xs_win[:].indirect(offs_t[:]))
         nc.vector.tensor_copy(staged[:, H + S :], xs_win[:].indirect(two_t[:]))
         for i in range(4):
-            queue = nc.scalar if i % 2 == 0 else nc.sync
-            queue.dma_start(planes[i:P:32, :].bitcast(I32), staged[8 * i : P : 32, :].bitcast(I32))
+            nc.scalar.dma_start(planes[i:P:32, :].bitcast(I32), staged[8 * i : P : 32, :].bitcast(I32))
 
         d_picked = tile("d_picked", H, U32, tag="xs_win")
         nc.vector.tensor_copy(d_picked[:], d_win[:].indirect(k1_t[:]))
         keys = tile("keys", H, U32)
         nc.vector.tensor_copy(keys[:].rearrange("p (t m) -> p m t", t=4), d_picked[:].rearrange("p (m t) -> p m t", t=4))
-        xa = tile("xa", S, U32, tag="xs_win")
-        nc.vector.tensor_copy(xa[:], x_win[:].indirect(offs_t[:]))
-        keys_s = tile("keys_s", H, U8)
+        xa = tile("xa", S, U32)
+        xb = tile("xb", S, U32)
+        keys_s = tile("keys_s", H, U8, tag="xs_win")
 
         def deal_key_scales(u):
             nc.vector.tensor_copy(
@@ -80,19 +77,19 @@ def tile_picked_twksmaxbover_none_po_kernel(
                 planes[:, 0:H].rearrange("p (m t) -> p m t", t=4)[:, :, 2 * u : 2 * u + 2],
             )
 
+        nc.vector.tensor_copy(xa[:], x_win[:].indirect(offs_t[:]))
         deal_key_scales(0)
-        xb = tile("xb", S, U32)
         nc.vector.tensor_copy(xb[:], x_win[:].indirect(two_t[:]))
         deal_key_scales(1)
 
         w1w_raw = tile("w1w_raw", 2 * N, U8, tag="d_win")
-        w1s_raw = tile("w1s_raw", N, U8, tag="staged")
+        w1s_raw = tile("w1s_raw", N, U8)
         gain = tile("gain", 4, F32)
+        nc.gpsimd.dma_start(gain[:], gn.rearrange("(p t) o -> p (t o)", t=4))
+        nc.sync.dma_start(w1w_raw[:].bitcast(I32), w1_words[0].bitcast(I32))
         nc.gpsimd.memset(w1s_raw[:].bitcast(I32), 0)
         for q in range(4):
-            nc.sync.dma_start(w1s_raw[32 * q : 32 * q + 4, :].bitcast(I32), w1_scales[0, 4 * q : 4 * q + 4, :].bitcast(I32))
-        nc.sync.dma_start(w1w_raw[:].bitcast(I32), w1_words[0].bitcast(I32))
-        nc.gpsimd.dma_start(gain[:], gn.rearrange("(p t) o -> p (t o)", t=4))
+            nc.gpsimd.dma_start(w1s_raw[32 * q : 32 * q + 4, :].bitcast(I32), w1_scales[0, 4 * q : 4 * q + 4, :].bitcast(I32))
 
         a_ps = [ps.tile([P, 2 * S], F32, name=f"a_ps{u}") for u in range(2)]
         b_ps = [ps.tile([P, 2 * S], F32, name=f"b_ps{u}") for u in range(2)]
@@ -111,7 +108,7 @@ def tile_picked_twksmaxbover_none_po_kernel(
                     )
 
         w1w = [tile("w1w_first", 2 * P, U8, tag="x_win")[:]]
-        w1s = [tile("w1s_first", P, U8, tag="xs_win")[:]]
+        w1s = [tile("w1s_first", P, U8, tag="xa")[:]]
 
         def deal_w1(t):
             nc.vector.tensor_copy(
@@ -185,32 +182,30 @@ def tile_picked_twksmaxbover_none_po_kernel(
 
         nc.scalar.activation(a_sb[0][:, 0 : 2 * S], a_ps[0][:], COPY, scale=0.0625)
         nc.vector.tensor_scalar(b_sb[0][:, 0 : 2 * S], b_ps[0][:], 0.0625, None, ALU.mult)
-        nc.scalar.activation(a_sb[1][:, 0 : 2 * S], a_ps[1][:], COPY, scale=0.0625)
-        fetch(nc.vector, a_n1, a_sb, n1_t, 0, 0, S)
-        nc.vector.tensor_scalar(b_sb[1][:, 0 : 2 * S], b_ps[1][:], 0.0625, None, ALU.mult)
-        fetch(nc.scalar, a_n1, a_sb, n1_t, 1, 0, S)
+        fetch(nc.scalar, a_n1, a_sb, n1_t, 0, 0, S)
+        fetch(nc.vector, a_n1, a_sb, n1_t, 1, 0, S)
         fetch(nc.scalar, b_n2, b_sb, n2_t, 0, 0, S)
         fetch(nc.scalar, b_n2, b_sb, n2_t, 1, 0, S)
+        nc.vector.tensor_scalar(a_sb[1][:, 0 : 2 * S], a_ps[1][:], 0.0625, None, ALU.mult)
+        nc.vector.tensor_scalar(b_sb[1][:, 0 : 2 * S], b_ps[1][:], 0.0625, None, ALU.mult)
+        for t in (2, 3):
+            fetch(nc.scalar, a_n1, a_sb, n1_t, t, 0, S)
+        for t in (2, 3):
+            fetch(nc.scalar, b_n2, b_sb, n2_t, t, 0, S)
         take_min(0, 0, S)
         take_max(0, 0, S)
-        for lo in (0, HALF):
-            for t in (2, 3):
-                fetch(nc.scalar, a_n1, a_sb, n1_t, t, lo, lo + HALF)
-            for t in (2, 3):
-                fetch(nc.scalar, b_n2, b_sb, n2_t, t, lo, lo + HALF)
-        take_min(1, 0, HALF)
+        take_min(1, 0, S)
         take_diff(0, 0, S)
-        take_max(1, 0, HALF)
-        take_min(1, HALF, S)
-        take_diff(1, 0, HALF)
-        take_max(1, HALF, S)
-        round_z(0, HALF)
-        take_diff(1, HALF, S)
+        for lo in (0, HALF):
+            take_max(1, lo, lo + HALF)
+        for lo in (0, HALF):
+            take_diff(1, lo, lo + HALF)
+        for lo in (0, HALF):
+            round_z(lo, lo + HALF)
         quantise_z(0, HALF)
-        round_z(HALF, S)
+        quantise_z(HALF, S)
         h_ps = layer(0, 0, HALF, "h0_lo")
         nc.scalar.copy(h_sb[0][:, 0:HALF], h_ps[:])
-        quantise_z(HALF, S)
         h_ps = layer(0, HALF, S, "h0_hi")
         nc.scalar.copy(h_sb[0][:, HALF:S], h_ps[:])
         w1w_rest = tile("w1w_rest", 6 * P, U8, tag="diff")

@@ -63,15 +63,18 @@ def tile_picked_twksmaxbover_none_po_kernel(
         for i in range(4):
             nc.scalar.dma_start(planes[i:P:32, :].bitcast(I32), staged[8 * i : P : 32, :].bitcast(I32))
 
-        d_picked = tile("d_picked", H, U32, tag="xs_win")
+        d_picked = tile("d_picked", H, U32, tag="ds_win")
         nc.vector.tensor_copy(d_picked[:], d_win[:].indirect(k1_t[:]))
         keys = tile("keys", H, U32)
-        nc.vector.tensor_copy(keys[:].rearrange("p (t m) -> p m t", t=4), d_picked[:].rearrange("p (m t) -> p m t", t=4))
         xa = tile("xa", S, U32)
         xb = tile("xb", S, U32)
-        keys_s = tile("keys_s", H, U8, tag="xs_win")
+        keys_s = tile("keys_s", H, U8, tag="d_win")
 
         def deal_key_scales(u):
+            nc.vector.tensor_copy(
+                keys[:, 2 * P * u : 2 * P * (u + 1)].rearrange("p (e m) -> p m e", e=2),
+                d_picked[:].rearrange("p (m t) -> p m t", t=4)[:, :, 2 * u : 2 * u + 2],
+            )
             nc.vector.tensor_copy(
                 keys_s[:, 2 * P * u : 2 * P * (u + 1)].rearrange("p (e m) -> p m e", e=2),
                 planes[:, 0:H].rearrange("p (m t) -> p m t", t=4)[:, :, 2 * u : 2 * u + 2],
@@ -82,7 +85,7 @@ def tile_picked_twksmaxbover_none_po_kernel(
         nc.vector.tensor_copy(xb[:], x_win[:].indirect(two_t[:]))
         deal_key_scales(1)
 
-        w1w_raw = tile("w1w_raw", 2 * N, U8, tag="d_win")
+        w1w_raw = tile("w1w_raw", 2 * N, U8, tag="xs_win")
         w1s_raw = tile("w1s_raw", N, U8)
         gain = tile("gain", 4, F32)
         nc.gpsimd.dma_start(gain[:], gn.rearrange("(p t) o -> p (t o)", t=4))
@@ -108,16 +111,18 @@ def tile_picked_twksmaxbover_none_po_kernel(
                     )
 
         w1w = [tile("w1w_first", 2 * P, U8, tag="x_win")[:]]
-        w1s = [tile("w1s_first", P, U8, tag="xa")[:]]
+        w1s = []
 
-        def deal_w1(t):
+        def deal_w1_words(t):
             nc.vector.tensor_copy(
                 w1w[t].rearrange("p (m b) -> p m b", b=2),
                 w1w_raw[:].rearrange("p (m t b) -> p m t b", t=4, b=2)[:, :, t, :],
             )
+
+        def deal_w1_scales(t):
             nc.vector.tensor_copy(w1s[t], w1s_raw[:].rearrange("p (m t) -> p m t", t=4)[:, :, t])
 
-        deal_w1(0)
+        deal_w1_words(0)
 
         a_sb = [tile(f"a_sb{u}", 3 * S, F32) for u in range(2)]
         b_sb = [tile(f"b_sb{u}", 3 * S, F32) for u in range(2)]
@@ -202,6 +207,8 @@ def tile_picked_twksmaxbover_none_po_kernel(
             take_diff(1, lo, lo + HALF)
         for lo in (0, HALF):
             round_z(lo, lo + HALF)
+        w1s.append(tile("w1s_first", P, U8, tag="larger")[:])
+        deal_w1_scales(0)
         quantise_z(0, HALF)
         quantise_z(HALF, S)
         h_ps = layer(0, 0, HALF, "h0_lo")
@@ -213,7 +220,8 @@ def tile_picked_twksmaxbover_none_po_kernel(
         for t in range(1, 4):
             w1w.append(w1w_rest[:, 2 * P * (t - 1) : 2 * P * t])
             w1s.append(w1s_rest[:, P * (t - 1) : P * t])
-            deal_w1(t)
+            deal_w1_words(t)
+            deal_w1_scales(t)
             h_ps = layer(t, 0, S, ["", "h1", "h2", "a_ps0"][t])
             nc.vector.tensor_copy(h_sb[t][:, 0:S], h_ps[:])
 

@@ -17,6 +17,15 @@ ALU = mybir.AluOpType
 COPY = mybir.ActivationFunctionType.Copy
 
 P = 128
+TILES = 4
+LIST_GROUP = 16
+BLOCKS = 16
+BLOCK_PARTS = 8
+QUADRANT = 32
+HALF = S // 2
+SCORE_SCALE = 0.0625
+RESIDUAL = -0.75
+VECTOR_CLEARS = 320
 
 
 def tile_picked_twksmaxbover_none_po_kernel(
@@ -31,9 +40,9 @@ def tile_picked_twksmaxbover_none_po_kernel(
             return sb.tile([P, cols], dtype, name=name, tag=tag or name, align_bytes=64)
 
         def load_list(name, src):
-            t = sb.tile([P, src.shape[1]], U16, name=name)
-            nc.sync.dma_start(t[:], src)
-            return t
+            offsets = sb.tile([P, src.shape[1]], U16, name=name)
+            nc.sync.dma_start(offsets[:], src)
+            return offsets
 
         d_win = tile("d_win", G, U32)
         x_win = tile("x_win", T, U32)
@@ -41,11 +50,12 @@ def tile_picked_twksmaxbover_none_po_kernel(
         xs_win = tile("xs_win", T, U8)
         planes = tile("planes", H + 2 * S, U8)
 
-        nc.vector.memset(ds_win[:].bitcast(I32), 0)
-        nc.gpsimd.memset(xs_win[:].bitcast(I32), 0)
+        nc.vector.memset(xs_win[:].bitcast(I32)[:, 0:VECTOR_CLEARS], 0)
+        nc.gpsimd.memset(xs_win[:].bitcast(I32)[:, VECTOR_CLEARS:], 0)
+        d_rows = d_scales[0].bitcast(I32)
+        nc.sync.dma_start(ds_win[:].bitcast(I32), d_rows.unsqueeze(1).to_broadcast([BLOCKS, BLOCK_PARTS, G // 4]))
         k1_t = load_list("k1_t", k1)
-        nc.scalar.dma_start(ds_win[0:P:8, :].bitcast(I32), d_scales[0].bitcast(I32))
-        nc.scalar.dma_start(xs_win[0:P:8, :].bitcast(I32), x_scales[0].bitcast(I32))
+        nc.scalar.dma_start(xs_win[0:P:BLOCK_PARTS, :].bitcast(I32), x_scales[0].bitcast(I32))
         offs_t = load_list("offs_t", offs)
         two_t = load_list("two_t", two)
         n1_t = load_list("n1_t", n1)
@@ -56,12 +66,13 @@ def tile_picked_twksmaxbover_none_po_kernel(
         n4_t = load_list("n4_t", n4)
         nc.vector.memset(planes[:].bitcast(I32), 0)
 
-        staged = tile("staged", H + 2 * S, U8)
-        nc.vector.tensor_copy(staged[:, 0:H], ds_win[:].indirect(k1_t[:]))
-        nc.vector.tensor_copy(staged[:, H : H + S], xs_win[:].indirect(offs_t[:]))
-        nc.vector.tensor_copy(staged[:, H + S :], xs_win[:].indirect(two_t[:]))
+        picked_s = tile("picked_s", H + 2 * S, U8)
+        nc.vector.tensor_copy(picked_s[:, 0:H], ds_win[:].indirect(k1_t[:]))
+        nc.vector.tensor_copy(picked_s[:, H : H + S], xs_win[:].indirect(offs_t[:]))
+        nc.vector.tensor_copy(picked_s[:, H + S :], xs_win[:].indirect(two_t[:]))
         for i in range(4):
-            nc.scalar.dma_start(planes[i:P:32, :].bitcast(I32), staged[8 * i : P : 32, :].bitcast(I32))
+            queue = nc.scalar if i % 2 == 0 else nc.sync
+            queue.dma_start(planes[i:P:QUADRANT, :].bitcast(I32), picked_s[BLOCK_PARTS * i : P : QUADRANT, :].bitcast(I32))
 
         d_picked = tile("d_picked", H, U32, tag="ds_win")
         nc.vector.tensor_copy(d_picked[:], d_win[:].indirect(k1_t[:]))
@@ -70,29 +81,28 @@ def tile_picked_twksmaxbover_none_po_kernel(
         xb = tile("xb", S, U32)
         keys_s = tile("keys_s", H, U8, tag="d_win")
 
-        def deal_key_scales(u):
-            nc.vector.tensor_copy(
-                keys[:, 2 * P * u : 2 * P * (u + 1)].rearrange("p (e m) -> p m e", e=2),
-                d_picked[:].rearrange("p (m t) -> p m t", t=4)[:, :, 2 * u : 2 * u + 2],
-            )
-            nc.vector.tensor_copy(
-                keys_s[:, 2 * P * u : 2 * P * (u + 1)].rearrange("p (e m) -> p m e", e=2),
-                planes[:, 0:H].rearrange("p (m t) -> p m t", t=4)[:, :, 2 * u : 2 * u + 2],
-            )
+        def deal_keys(u):
+            for dealt, picked in ((keys, d_picked[:]), (keys_s, planes[:, 0:H])):
+                nc.vector.tensor_copy(
+                    dealt[:, 2 * P * u : 2 * P * (u + 1)].rearrange("p (e m) -> p m e", e=2),
+                    picked.rearrange("p (m t) -> p m t", t=TILES)[:, :, 2 * u : 2 * u + 2],
+                )
 
         nc.vector.tensor_copy(xa[:], x_win[:].indirect(offs_t[:]))
-        deal_key_scales(0)
+        deal_keys(0)
         nc.vector.tensor_copy(xb[:], x_win[:].indirect(two_t[:]))
-        deal_key_scales(1)
+        deal_keys(1)
 
         w1w_raw = tile("w1w_raw", 2 * N, U8, tag="xs_win")
         w1s_raw = tile("w1s_raw", N, U8)
-        gain = tile("gain", 4, F32)
-        nc.gpsimd.dma_start(gain[:], gn.rearrange("(p t) o -> p (t o)", t=4))
+        gain = tile("gain", TILES, F32)
+        nc.gpsimd.dma_start(gain[:], gn.rearrange("(p t) o -> p (t o)", t=TILES))
         nc.sync.dma_start(w1w_raw[:].bitcast(I32), w1_words[0].bitcast(I32))
         nc.gpsimd.memset(w1s_raw[:].bitcast(I32), 0)
         for q in range(4):
-            nc.gpsimd.dma_start(w1s_raw[32 * q : 32 * q + 4, :].bitcast(I32), w1_scales[0, 4 * q : 4 * q + 4, :].bitcast(I32))
+            nc.gpsimd.dma_start(
+                w1s_raw[QUADRANT * q : QUADRANT * q + 4, :].bitcast(I32), w1_scales[0, 4 * q : 4 * q + 4, :].bitcast(I32)
+            )
 
         a_ps = [ps.tile([P, 2 * S], F32, name=f"a_ps{u}") for u in range(2)]
         b_ps = [ps.tile([P, 2 * S], F32, name=f"b_ps{u}") for u in range(2)]
@@ -116,11 +126,11 @@ def tile_picked_twksmaxbover_none_po_kernel(
         def deal_w1_words(t):
             nc.vector.tensor_copy(
                 w1w[t].rearrange("p (m b) -> p m b", b=2),
-                w1w_raw[:].rearrange("p (m t b) -> p m t b", t=4, b=2)[:, :, t, :],
+                w1w_raw[:].rearrange("p (m t b) -> p m t b", t=TILES, b=2)[:, :, t, :],
             )
 
         def deal_w1_scales(t):
-            nc.vector.tensor_copy(w1s[t], w1s_raw[:].rearrange("p (m t) -> p m t", t=4)[:, :, t])
+            nc.vector.tensor_copy(w1s[t], w1s_raw[:].rearrange("p (m t) -> p m t", t=TILES)[:, :, t])
 
         deal_w1_words(0)
 
@@ -128,52 +138,48 @@ def tile_picked_twksmaxbover_none_po_kernel(
         b_sb = [tile(f"b_sb{u}", 3 * S, F32) for u in range(2)]
         a_n1 = [tile(f"a_n1_{u}", 2 * S, F32) for u in range(2)]
         b_n2 = [tile(f"b_n2_{u}", 2 * S, F32) for u in range(2)]
-        larger = tile("larger", 4 * S, F32)
-        smaller = tile("smaller", 4 * S, F32)
-        diff = tile("diff", 4 * S, F32)
-        z = tile("z", 4 * S, BF16)
+        larger = tile("larger", TILES * S, F32)
+        smaller = tile("smaller", TILES * S, F32)
+        diff = tile("diff", TILES * S, F32)
+        z = tile("z", TILES * S, BF16)
         z_codes = tile("z_codes", S, U32)
         z_scales = tile("z_scales", S, U8)
-        h_sb = [tile(f"h_sb{t}", 2 * S, F32) for t in range(4)]
-        HALF = S // 2
+        h_sb = [tile(f"h_sb{t}", 2 * S, F32) for t in range(TILES)]
 
-        def fetch(engine, dst, src, lst, t, lo, hi):
+        def look_up(scores, offsets, t):
             u, e = divmod(t, 2)
-            window = src[u][:, S * e : S * (e + 2)].indirect(lst[:, lo // 16 : hi // 16])
-            out = dst[u][:, S * e + lo : S * e + hi]
-            if engine is nc.vector:
-                nc.vector.tensor_copy(out, window)
-            else:
-                nc.scalar.activation(out, window, COPY)
+            return scores[u][:, S * e : S * (e + 2)].indirect(offsets[:])
 
-        def part(ap, u, lo, hi):
-            return ap[:, 0 : 2 * S].rearrange("p (e j) -> p e j", e=2)[:, :, lo:hi]
+        def row_of(pairs, t):
+            u, e = divmod(t, 2)
+            return pairs[u][:, S * e : S * (e + 1)]
 
-        def wide(t_, u, lo, hi):
-            return t_[:, 2 * S * u : 2 * S * (u + 1)].rearrange("p (e j) -> p e j", e=2)[:, :, lo:hi]
+        def places(values, first, lo, hi):
+            return values[:, first : first + 2 * S].rearrange("p (e j) -> p e j", e=2)[:, :, lo:hi]
 
         def take_max(u, lo, hi):
-            nc.vector.tensor_tensor(wide(larger, u, lo, hi), part(a_sb[u], u, lo, hi), part(b_n2[u], u, lo, hi), ALU.max)
+            nc.vector.tensor_tensor(places(larger, 2 * S * u, lo, hi), places(a_sb[u], 0, lo, hi), places(b_n2[u], 0, lo, hi), ALU.max)
 
         def take_min(u, lo, hi):
-            nc.vector.tensor_tensor(wide(smaller, u, lo, hi), part(a_n1[u], u, lo, hi), part(b_sb[u], u, lo, hi), ALU.min)
+            nc.vector.tensor_tensor(places(smaller, 2 * S * u, lo, hi), places(a_n1[u], 0, lo, hi), places(b_sb[u], 0, lo, hi), ALU.min)
 
         def take_diff(u, lo, hi):
-            nc.vector.tensor_tensor(wide(diff, u, lo, hi), wide(larger, u, lo, hi), wide(smaller, u, lo, hi), ALU.subtract)
+            first = 2 * S * u
+            nc.vector.tensor_tensor(places(diff, first, lo, hi), places(larger, first, lo, hi), places(smaller, first, lo, hi), ALU.subtract)
 
         def round_z(lo, hi):
             nc.vector.tensor_tensor(
-                z[:, 4 * lo : 4 * hi].rearrange("p (c i t) -> p c t i", i=4, t=4),
-                diff[:].rearrange("p (t c i) -> p c t i", i=4, t=4)[:, lo // 4 : hi // 4, :, :],
-                gain[:].unsqueeze(1).unsqueeze(3).to_broadcast([P, (hi - lo) // 4, 4, 4]),
+                z[:, TILES * lo : TILES * hi].rearrange("p (c i t) -> p c t i", i=4, t=TILES),
+                diff[:].rearrange("p (t c i) -> p c t i", i=4, t=TILES)[:, lo // 4 : hi // 4, :, :],
+                gain[:].unsqueeze(1).unsqueeze(3).to_broadcast([P, (hi - lo) // 4, TILES, 4]),
                 ALU.mult,
             )
 
         def quantise_z(lo, hi):
-            nc.vector.quantize_mx(out=z_codes[:, lo:hi].bitcast(FP8X4), scales=z_scales[:, lo:hi], in_=z[:, 4 * lo : 4 * hi])
+            nc.vector.quantize_mx(out=z_codes[:, lo:hi].bitcast(FP8X4), scales=z_scales[:, lo:hi], in_=z[:, TILES * lo : TILES * hi])
 
-        def layer(t, lo, hi, tag):
-            h_ps = ps.tile([P, hi - lo], F32, name=f"h_ps{t}_{lo}", tag=tag)
+        def layer(t, lo, hi, bank):
+            h_ps = ps.tile([P, hi - lo], F32, name=f"h_ps{t}_{lo}", tag=bank)
             nc.tensor.matmul_mx(
                 out=h_ps[:],
                 lhsT=w1w[t].bitcast(FP4X4),
@@ -185,18 +191,18 @@ def tile_picked_twksmaxbover_none_po_kernel(
             )
             return h_ps
 
-        nc.scalar.activation(a_sb[0][:, 0 : 2 * S], a_ps[0][:], COPY, scale=0.0625)
-        nc.vector.tensor_scalar(b_sb[0][:, 0 : 2 * S], b_ps[0][:], 0.0625, None, ALU.mult)
-        fetch(nc.scalar, a_n1, a_sb, n1_t, 0, 0, S)
-        fetch(nc.vector, a_n1, a_sb, n1_t, 1, 0, S)
-        fetch(nc.scalar, b_n2, b_sb, n2_t, 0, 0, S)
-        fetch(nc.scalar, b_n2, b_sb, n2_t, 1, 0, S)
-        nc.vector.tensor_scalar(a_sb[1][:, 0 : 2 * S], a_ps[1][:], 0.0625, None, ALU.mult)
-        nc.vector.tensor_scalar(b_sb[1][:, 0 : 2 * S], b_ps[1][:], 0.0625, None, ALU.mult)
+        nc.scalar.activation(a_sb[0][:, 0 : 2 * S], a_ps[0][:], COPY, scale=SCORE_SCALE)
+        nc.vector.tensor_scalar(b_sb[0][:, 0 : 2 * S], b_ps[0][:], SCORE_SCALE, None, ALU.mult)
+        nc.scalar.activation(row_of(a_n1, 0), look_up(a_sb, n1_t, 0), COPY)
+        nc.vector.tensor_copy(row_of(a_n1, 1), look_up(a_sb, n1_t, 1))
+        for t in (0, 1):
+            nc.scalar.activation(row_of(b_n2, t), look_up(b_sb, n2_t, t), COPY)
+        nc.vector.tensor_scalar(a_sb[1][:, 0 : 2 * S], a_ps[1][:], SCORE_SCALE, None, ALU.mult)
+        nc.vector.tensor_scalar(b_sb[1][:, 0 : 2 * S], b_ps[1][:], SCORE_SCALE, None, ALU.mult)
         for t in (2, 3):
-            fetch(nc.scalar, a_n1, a_sb, n1_t, t, 0, S)
+            nc.scalar.activation(row_of(a_n1, t), look_up(a_sb, n1_t, t), COPY)
         for t in (2, 3):
-            fetch(nc.scalar, b_n2, b_sb, n2_t, t, 0, S)
+            nc.scalar.activation(row_of(b_n2, t), look_up(b_sb, n2_t, t), COPY)
         take_min(0, 0, S)
         take_max(0, 0, S)
         take_min(1, 0, S)
@@ -209,36 +215,37 @@ def tile_picked_twksmaxbover_none_po_kernel(
             round_z(lo, lo + HALF)
         w1s.append(tile("w1s_first", P, U8, tag="larger")[:])
         deal_w1_scales(0)
-        quantise_z(0, HALF)
-        quantise_z(HALF, S)
-        h_ps = layer(0, 0, HALF, "h0_lo")
-        nc.scalar.copy(h_sb[0][:, 0:HALF], h_ps[:])
-        h_ps = layer(0, HALF, S, "h0_hi")
-        nc.scalar.copy(h_sb[0][:, HALF:S], h_ps[:])
-        w1w_rest = tile("w1w_rest", 6 * P, U8, tag="diff")
-        w1s_rest = tile("w1s_rest", 3 * P, U8, tag="gain")
-        for t in range(1, 4):
+        for lo in (0, HALF):
+            quantise_z(lo, lo + HALF)
+
+        for lo in (0, HALF):
+            h_ps = layer(0, lo, lo + HALF, f"h0_{lo}")
+            nc.scalar.copy(h_sb[0][:, lo : lo + HALF], h_ps[:])
+        w1w_rest = tile("w1w_rest", 2 * P * (TILES - 1), U8, tag="diff")
+        w1s_rest = tile("w1s_rest", P * (TILES - 1), U8, tag="gain")
+        for t, bank in ((1, "h1"), (2, "h2"), (3, "a_ps0")):
             w1w.append(w1w_rest[:, 2 * P * (t - 1) : 2 * P * t])
             w1s.append(w1s_rest[:, P * (t - 1) : P * t])
             deal_w1_words(t)
             deal_w1_scales(t)
-            h_ps = layer(t, 0, S, ["", "h1", "h2", "a_ps0"][t])
+            h_ps = layer(t, 0, S, bank)
             nc.vector.tensor_copy(h_sb[t][:, 0:S], h_ps[:])
 
-        y = tile("y", 4 * S, F32)
-        y_bf = tile("y_bf", 4 * S, BF16)
+        y = tile("y", TILES * S, F32)
+        y_bf = tile("y_bf", TILES * S, BF16)
         y_codes = tile("y_codes", S, U32)
         y_scales = tile("y_scales", S, U8)
-        h_n3 = tile("h_n3", 4 * S, F32)
-        h_n4 = tile("h_n4", 4 * S, F32)
-        top = tile("top", 4 * S, F32)
-        out_rows = out_0.rearrange("(p t) j -> p t j", t=4)
+        h_n3 = tile("h_n3", TILES * S, F32)
+        h_n4 = tile("h_n4", TILES * S, F32)
+        top = tile("top", TILES * S, F32)
+        out_rows = out_0.rearrange("(p t) j -> p t j", t=TILES)
         out_words = out_1[0].rearrange("p n t -> p (n t)").bitcast(I32)
 
         def fetch_h(t, lo, hi):
             cols = slice(S * t + lo, S * t + hi)
-            nc.scalar.activation(h_n3[:, cols], h_sb[t][:].indirect(n3_t[:, lo // 16 : hi // 16]), COPY)
-            nc.scalar.activation(h_n4[:, cols], h_sb[t][:].indirect(n4_t[:, lo // 16 : hi // 16]), COPY)
+            entries = slice(lo // LIST_GROUP, hi // LIST_GROUP)
+            nc.scalar.activation(h_n3[:, cols], h_sb[t][:].indirect(n3_t[:, entries]), COPY)
+            nc.scalar.activation(h_n4[:, cols], h_sb[t][:].indirect(n4_t[:, entries]), COPY)
 
         def take_top(t, lo, hi):
             cols = slice(S * t + lo, S * t + hi)
@@ -246,25 +253,28 @@ def tile_picked_twksmaxbover_none_po_kernel(
 
         def take_y(t, lo, hi):
             cols = slice(S * t + lo, S * t + hi)
-            nc.vector.scalar_tensor_tensor(y[:, cols], h_sb[t][:, lo:hi], -0.75, top[:, cols], ALU.mult, ALU.add)
+            nc.vector.scalar_tensor_tensor(y[:, cols], h_sb[t][:, lo:hi], RESIDUAL, top[:, cols], ALU.mult, ALU.add)
 
         def round_y(t, lo, hi):
             nc.vector.tensor_copy(
-                y_bf[:].rearrange("p (j t) -> p j t", t=4)[:, lo:hi, t : t + 2],
-                y[:].rearrange("p (t j) -> p j t", t=4)[:, lo:hi, t : t + 2],
+                y_bf[:].rearrange("p (j t) -> p j t", t=TILES)[:, lo:hi, t : t + 2],
+                y[:].rearrange("p (t j) -> p j t", t=TILES)[:, lo:hi, t : t + 2],
             )
 
         def quantise_y(lo, hi):
-            nc.vector.quantize_mx(out=y_codes[:, lo:hi].bitcast(FP8X4), scales=y_scales[:, lo:hi], in_=y_bf[:, 4 * lo : 4 * hi])
+            nc.vector.quantize_mx(out=y_codes[:, lo:hi].bitcast(FP8X4), scales=y_scales[:, lo:hi], in_=y_bf[:, TILES * lo : TILES * hi])
             nc.sync.dma_start(out_words[:, lo:hi], y_codes[:, lo:hi].bitcast(I32))
 
-        for t in range(3):
+        def whole_tile(t):
             fetch_h(t, 0, S)
             take_top(t, 0, S)
             take_y(t, 0, S)
             nc.sync.dma_start(out_rows[:, t, :], y[:, S * t : S * (t + 1)])
-            if t == 1:
-                round_y(0, 0, S)
+
+        whole_tile(0)
+        whole_tile(1)
+        round_y(0, 0, S)
+        whole_tile(2)
         fetch_h(3, 0, HALF)
         fetch_h(3, HALF, S)
         take_top(3, 0, HALF)
@@ -278,4 +288,4 @@ def tile_picked_twksmaxbover_none_po_kernel(
         quantise_y(HALF, S)
         for q in range(4):
             queue = nc.scalar if q % 2 == 0 else nc.sync
-            queue.dma_start(out_2[0, 4 * q : 4 * q + 4, :].bitcast(I32), y_scales[32 * q : 32 * q + 4, :].bitcast(I32))
+            queue.dma_start(out_2[0, 4 * q : 4 * q + 4, :].bitcast(I32), y_scales[QUADRANT * q : QUADRANT * q + 4, :].bitcast(I32))

from contextlib import ExitStack

import concourse.mybir as mybir

K, T, S, N, G, H = 512, 2048, 256, 512, 2048, 512
FLOPS = 2 * K * H * S * 2 + 2 * H * N * S

F32 = mybir.dt.float32
BF16 = mybir.dt.bfloat16
I32 = mybir.dt.int32
U32 = mybir.dt.uint32
U16 = mybir.dt.uint16
U8 = mybir.dt.uint8
FP8X4 = mybir.dt.float8_e4m3fn_x4
FP4X4 = mybir.dt.float4_e2m1fn_x4
ALU = mybir.AluOpType
COPY = mybir.ActivationFunctionType.Copy

P = 128
TILES = 4
LIST_GROUP = 16
BLOCKS = 16
BLOCK_PARTS = 8
QUADRANT = 32
HALF = S // 2
SCORE_SCALE = 0.0625
RESIDUAL = -0.75
VECTOR_CLEARS = 320


def tile_picked_twksmaxbover_none_po_kernel(
    tc, x_words, x_scales, d_words, d_scales, gn, w1_words, w1_scales, offs, k1, two, n1, n2, n3, n4, out_0, out_1, out_2
):
    nc = tc.nc
    with ExitStack() as ctx:
        sb = ctx.enter_context(tc.tile_pool(name="sb", bufs=1))
        ps = ctx.enter_context(tc.psum_pool(name="ps", bufs=1))

        def tile(name, cols, dtype, tag=None):
            return sb.tile([P, cols], dtype, name=name, tag=tag or name, align_bytes=64)

        def load_list(name, src):
            offsets = sb.tile([P, src.shape[1]], U16, name=name)
            nc.sync.dma_start(offsets[:], src)
            return offsets

        d_win = tile("d_win", G, U32)
        x_win = tile("x_win", T, U32)
        ds_win = tile("ds_win", G, U8)
        xs_win = tile("xs_win", T, U8)
        planes = tile("planes", H + 2 * S, U8)

        nc.vector.memset(xs_win[:].bitcast(I32)[:, 0:VECTOR_CLEARS], 0)
        nc.gpsimd.memset(xs_win[:].bitcast(I32)[:, VECTOR_CLEARS:], 0)
        d_rows = d_scales[0].bitcast(I32)
        nc.sync.dma_start(ds_win[:].bitcast(I32), d_rows.unsqueeze(1).to_broadcast([BLOCKS, BLOCK_PARTS, G // 4]))
        k1_t = load_list("k1_t", k1)
        nc.scalar.dma_start(xs_win[0:P:BLOCK_PARTS, :].bitcast(I32), x_scales[0].bitcast(I32))
        offs_t = load_list("offs_t", offs)
        two_t = load_list("two_t", two)
        n1_t = load_list("n1_t", n1)
        n2_t = load_list("n2_t", n2)
        nc.sync.dma_start(d_win[:].bitcast(I32), d_words[0].rearrange("p n t -> p (n t)").bitcast(I32))
        nc.sync.dma_start(x_win[:].bitcast(I32), x_words[0].rearrange("p n t -> p (n t)").bitcast(I32))
        n3_t = load_list("n3_t", n3)
        n4_t = load_list("n4_t", n4)
        nc.vector.memset(planes[:].bitcast(I32), 0)

        picked_s = tile("picked_s", H + 2 * S, U8)
        nc.vector.tensor_copy(picked_s[:, 0:H], ds_win[:].indirect(k1_t[:]))
        nc.vector.tensor_copy(picked_s[:, H : H + S], xs_win[:].indirect(offs_t[:]))
        nc.vector.tensor_copy(picked_s[:, H + S :], xs_win[:].indirect(two_t[:]))
        for i in range(4):
            queue = nc.scalar if i % 2 == 0 else nc.sync
            queue.dma_start(planes[i:P:QUADRANT, :].bitcast(I32), picked_s[BLOCK_PARTS * i : P : QUADRANT, :].bitcast(I32))

        d_picked = tile("d_picked", H, U32, tag="ds_win")
        nc.vector.tensor_copy(d_picked[:], d_win[:].indirect(k1_t[:]))
        keys = tile("keys", H, U32)
        xa = tile("xa", S, U32)
        xb = tile("xb", S, U32)
        keys_s = tile("keys_s", H, U8, tag="d_win")

        def deal_keys(u):
            for dealt, picked in ((keys, d_picked[:]), (keys_s, planes[:, 0:H])):
                nc.vector.tensor_copy(
                    dealt[:, 2 * P * u : 2 * P * (u + 1)].rearrange("p (e m) -> p m e", e=2),
                    picked.rearrange("p (m t) -> p m t", t=TILES)[:, :, 2 * u : 2 * u + 2],
                )

        nc.vector.tensor_copy(xa[:], x_win[:].indirect(offs_t[:]))
        deal_keys(0)
        nc.vector.tensor_copy(xb[:], x_win[:].indirect(two_t[:]))
        deal_keys(1)

        w1w_raw = tile("w1w_raw", 2 * N, U8, tag="xs_win")
        w1s_raw = tile("w1s_raw", N, U8)
        gain = tile("gain", TILES, F32)
        nc.gpsimd.dma_start(gain[:], gn.rearrange("(p t) o -> p (t o)", t=TILES))
        nc.sync.dma_start(w1w_raw[:].bitcast(I32), w1_words[0].bitcast(I32))
        nc.gpsimd.memset(w1s_raw[:].bitcast(I32), 0)
        for q in range(4):
            nc.gpsimd.dma_start(
                w1s_raw[QUADRANT * q : QUADRANT * q + 4, :].bitcast(I32), w1_scales[0, 4 * q : 4 * q + 4, :].bitcast(I32)
            )

        a_ps = [ps.tile([P, 2 * S], F32, name=f"a_ps{u}") for u in range(2)]
        b_ps = [ps.tile([P, 2 * S], F32, name=f"b_ps{u}") for u in range(2)]
        for u in range(2):
            for bank, tokens, first in ((a_ps[u], xa, H), (b_ps[u], xb, H + S)):
                for e in range(2):
                    cols = slice(P * (2 * u + e), P * (2 * u + e + 1))
                    nc.tensor.matmul_mx(
                        out=bank[:, S * e : S * (e + 1)],
                        lhsT=keys[:, cols].bitcast(FP8X4),
                        lhsT_scale=keys_s[:, cols],
                        rhs=tokens[:].bitcast(FP8X4),
                        rhs_scale=planes[:, first : first + S],
                        start=True,
                        stop=True,
                    )

        w1w = [tile("w1w_first", 2 * P, U8, tag="x_win")[:]]
        w1s = []

        def deal_w1_words(t):
            nc.vector.tensor_copy(
                w1w[t].rearrange("p (m b) -> p m b", b=2),
                w1w_raw[:].rearrange("p (m t b) -> p m t b", t=TILES, b=2)[:, :, t, :],
            )

        def deal_w1_scales(t):
            nc.vector.tensor_copy(w1s[t], w1s_raw[:].rearrange("p (m t) -> p m t", t=TILES)[:, :, t])

        deal_w1_words(0)

        a_sb = [tile(f"a_sb{u}", 3 * S, F32) for u in range(2)]
        b_sb = [tile(f"b_sb{u}", 3 * S, F32) for u in range(2)]
        a_n1 = [tile(f"a_n1_{u}", 2 * S, F32) for u in range(2)]
        b_n2 = [tile(f"b_n2_{u}", 2 * S, F32) for u in range(2)]
        larger = tile("larger", TILES * S, F32)
        smaller = tile("smaller", TILES * S, F32)
        diff = tile("diff", TILES * S, F32)
        z = tile("z", TILES * S, BF16)
        z_codes = tile("z_codes", S, U32)
        z_scales = tile("z_scales", S, U8)
        h_sb = [tile(f"h_sb{t}", 2 * S, F32) for t in range(TILES)]

        def look_up(scores, offsets, t):
            u, e = divmod(t, 2)
            return scores[u][:, S * e : S * (e + 2)].indirect(offsets[:])

        def row_of(pairs, t):
            u, e = divmod(t, 2)
            return pairs[u][:, S * e : S * (e + 1)]

        def places(values, first, lo, hi):
            return values[:, first : first + 2 * S].rearrange("p (e j) -> p e j", e=2)[:, :, lo:hi]

        def take_max(u, lo, hi):
            nc.vector.tensor_tensor(places(larger, 2 * S * u, lo, hi), places(a_sb[u], 0, lo, hi), places(b_n2[u], 0, lo, hi), ALU.max)

        def take_min(u, lo, hi):
            nc.vector.tensor_tensor(places(smaller, 2 * S * u, lo, hi), places(a_n1[u], 0, lo, hi), places(b_sb[u], 0, lo, hi), ALU.min)

        def take_diff(u, lo, hi):
            first = 2 * S * u
            nc.vector.tensor_tensor(places(diff, first, lo, hi), places(larger, first, lo, hi), places(smaller, first, lo, hi), ALU.subtract)

        def round_z(lo, hi):
            nc.vector.tensor_tensor(
                z[:, TILES * lo : TILES * hi].rearrange("p (c i t) -> p c t i", i=4, t=TILES),
                diff[:].rearrange("p (t c i) -> p c t i", i=4, t=TILES)[:, lo // 4 : hi // 4, :, :],
                gain[:].unsqueeze(1).unsqueeze(3).to_broadcast([P, (hi - lo) // 4, TILES, 4]),
                ALU.mult,
            )

        def quantise_z(lo, hi):
            nc.vector.quantize_mx(out=z_codes[:, lo:hi].bitcast(FP8X4), scales=z_scales[:, lo:hi], in_=z[:, TILES * lo : TILES * hi])

        def layer(t, lo, hi, bank):
            h_ps = ps.tile([P, hi - lo], F32, name=f"h_ps{t}_{lo}", tag=bank)
            nc.tensor.matmul_mx(
                out=h_ps[:],
                lhsT=w1w[t].bitcast(FP4X4),
                lhsT_scale=w1s[t],
                rhs=z_codes[:, lo:hi].bitcast(FP8X4),
                rhs_scale=z_scales[:, lo:hi],
                start=True,
                stop=True,
            )
            return h_ps

        nc.scalar.activation(a_sb[0][:, 0 : 2 * S], a_ps[0][:], COPY, scale=SCORE_SCALE)
        nc.vector.tensor_scalar(b_sb[0][:, 0 : 2 * S], b_ps[0][:], SCORE_SCALE, None, ALU.mult)
        nc.scalar.activation(row_of(a_n1, 0), look_up(a_sb, n1_t, 0), COPY)
        nc.vector.tensor_copy(row_of(a_n1, 1), look_up(a_sb, n1_t, 1))
        for t in (0, 1):
            nc.scalar.activation(row_of(b_n2, t), look_up(b_sb, n2_t, t), COPY)
        nc.vector.tensor_scalar(a_sb[1][:, 0 : 2 * S], a_ps[1][:], SCORE_SCALE, None, ALU.mult)
        nc.vector.tensor_scalar(b_sb[1][:, 0 : 2 * S], b_ps[1][:], SCORE_SCALE, None, ALU.mult)
        for t in (2, 3):
            nc.scalar.activation(row_of(a_n1, t), look_up(a_sb, n1_t, t), COPY)
        for t in (2, 3):
            nc.scalar.activation(row_of(b_n2, t), look_up(b_sb, n2_t, t), COPY)
        take_min(0, 0, S)
        take_max(0, 0, S)
        take_min(1, 0, S)
        take_diff(0, 0, S)
        for lo in (0, HALF):
            take_max(1, lo, lo + HALF)
        for lo in (0, HALF):
            take_diff(1, lo, lo + HALF)
        for lo in (0, HALF):
            round_z(lo, lo + HALF)
        w1s.append(tile("w1s_first", P, U8, tag="larger")[:])
        deal_w1_scales(0)
        for lo in (0, HALF):
            quantise_z(lo, lo + HALF)

        for lo in (0, HALF):
            h_ps = layer(0, lo, lo + HALF, f"h0_{lo}")
            nc.scalar.copy(h_sb[0][:, lo : lo + HALF], h_ps[:])
        w1w_rest = tile("w1w_rest", 2 * P * (TILES - 1), U8, tag="diff")
        w1s_rest = tile("w1s_rest", P * (TILES - 1), U8, tag="gain")
        for t, bank in ((1, "h1"), (2, "h2"), (3, "a_ps0")):
            w1w.append(w1w_rest[:, 2 * P * (t - 1) : 2 * P * t])
            w1s.append(w1s_rest[:, P * (t - 1) : P * t])
            deal_w1_words(t)
            deal_w1_scales(t)
            h_ps = layer(t, 0, S, bank)
            nc.vector.tensor_copy(h_sb[t][:, 0:S], h_ps[:])

        y = tile("y", TILES * S, F32)
        y_bf = tile("y_bf", TILES * S, BF16)
        y_codes = tile("y_codes", S, U32)
        y_scales = tile("y_scales", S, U8)
        h_n3 = tile("h_n3", TILES * S, F32)
        h_n4 = tile("h_n4", TILES * S, F32)
        top = tile("top", TILES * S, F32)
        out_rows = out_0.rearrange("(p t) j -> p t j", t=TILES)
        out_words = out_1[0].rearrange("p n t -> p (n t)").bitcast(I32)

        def fetch_h(t, lo, hi):
            cols = slice(S * t + lo, S * t + hi)
            entries = slice(lo // LIST_GROUP, hi // LIST_GROUP)
            nc.scalar.activation(h_n3[:, cols], h_sb[t][:].indirect(n3_t[:, entries]), COPY)
            nc.scalar.activation(h_n4[:, cols], h_sb[t][:].indirect(n4_t[:, entries]), COPY)

        def take_top(t, lo, hi):
            cols = slice(S * t + lo, S * t + hi)
            nc.vector.tensor_tensor(top[:, cols], h_n3[:, cols], h_n4[:, cols], ALU.max)

        def take_y(t, lo, hi):
            cols = slice(S * t + lo, S * t + hi)
            nc.vector.scalar_tensor_tensor(y[:, cols], h_sb[t][:, lo:hi], RESIDUAL, top[:, cols], ALU.mult, ALU.add)

        def round_y(t, lo, hi):
            nc.vector.tensor_copy(
                y_bf[:].rearrange("p (j t) -> p j t", t=TILES)[:, lo:hi, t : t + 2],
                y[:].rearrange("p (t j) -> p j t", t=TILES)[:, lo:hi, t : t + 2],
            )

        def quantise_y(lo, hi):
            nc.vector.quantize_mx(out=y_codes[:, lo:hi].bitcast(FP8X4), scales=y_scales[:, lo:hi], in_=y_bf[:, TILES * lo : TILES * hi])
            nc.sync.dma_start(out_words[:, lo:hi], y_codes[:, lo:hi].bitcast(I32))

        def whole_tile(t):
            fetch_h(t, 0, S)
            take_top(t, 0, S)
            take_y(t, 0, S)
            nc.sync.dma_start(out_rows[:, t, :], y[:, S * t : S * (t + 1)])

        whole_tile(0)
        whole_tile(1)
        round_y(0, 0, S)
        whole_tile(2)
        fetch_h(3, 0, HALF)
        fetch_h(3, HALF, S)
        take_top(3, 0, HALF)
        take_y(3, 0, HALF)
        take_top(3, HALF, S)
        round_y(2, 0, HALF)
        take_y(3, HALF, S)
        nc.scalar.dma_start(out_rows[:, 3, :], y[:, S * 3 : S * 4])
        quantise_y(0, HALF)
        round_y(2, HALF, S)
        quantise_y(HALF, S)
        for q in range(4):
            queue = nc.scalar if q % 2 == 0 else nc.sync
            queue.dma_start(out_2[0, 4 * q : 4 * q + 4, :].bitcast(I32), y_scales[QUADRANT * q : QUADRANT * q + 4, :].bitcast(I32))
